import numpy as np
import ml_dtypes


def mxq(x, axis, fmt="e4m3"):
    dtype, down = {"e4m3": (ml_dtypes.float8_e4m3fn, 7), "e5m2": (ml_dtypes.float8_e5m2, 14)}[fmt]
    v = np.moveaxis(np.asarray(x, np.float32).astype(ml_dtypes.bfloat16).astype(np.float64), axis, -1)
    blocks = v.reshape(v.shape[:-1] + (-1, 32))
    amax = np.abs(blocks).max(-1, keepdims=True)
    byte = np.maximum(np.where(amax > 0, np.frexp(amax)[1] - 1 + 127, 0) - down, 1)
    scale = np.exp2(byte - 127.0)
    codes = (blocks / scale).astype(np.float32).astype(dtype).astype(np.float64)
    return np.moveaxis((codes * scale).reshape(v.shape), -1, axis)


WIDE = False


def mx_kscale(k):
    if not WIDE:
        return np.ones(k)
    levels = np.array([10, -10, 5, -5, 0])
    if k % 512:
        return np.exp2(np.random.permutation(np.resize(levels, k // 32))).repeat(32)
    a = np.empty((k // 512, 16))
    for p in range(k // 512):
        a[p, :8] = np.random.permutation(np.resize(levels, 8))
        for g in range(8):
            far = levels[np.abs(levels - a[p, g]) >= 10]
            a[p, g + 8] = far[np.random.randint(len(far))]
    return np.exp2(a.ravel()).repeat(32)


def f64(x):
    return np.asarray(x).astype(np.float64)


def striped(idx):
    return np.tile(idx.reshape(-1, 16).T, (8, 1)).astype(np.uint16)


def unstriped(offs):
    return offs[:16].T.reshape(-1).astype(np.int64)


E2M1 = np.array([0.0, 0.5, 1.0, 1.5, 2.0, 3.0, 4.0, 6.0, -0.0, -0.5, -1.0, -1.5, -2.0, -3.0, -4.0, -6.0])


def pack_weight(w, fmt):
    k, n = w.shape
    w = f64(np.asarray(w, np.float32).astype(ml_dtypes.bfloat16)).reshape(k // 32, 32, n)
    amax = np.abs(w).max(1)
    if fmt == "e4m3":
        byte = np.frexp(amax)[1] - 1 + 127 - 7
    else:
        mant, ex = np.frexp(amax / 6.0)
        byte = np.where(mant > 0.5, ex, ex - 1) + 127
    byte = np.clip(np.where(amax > 0, byte, 1), 1, 254)
    scaled = (w * np.exp2(127.0 - byte)[:, None, :]).reshape(k, n).astype(np.float32)
    by_word = np.ascontiguousarray(scaled.reshape(k // 512, 128, 4, n).transpose(0, 1, 3, 2))
    if fmt == "e4m3":
        words = by_word.astype(ml_dtypes.float8_e4m3fn).view(np.uint8)
    else:
        c = by_word.astype(ml_dtypes.float4_e2m1fn).view(np.uint8) & 0xF
        words = (c[..., 0::2] | (c[..., 1::2] << 4)).reshape(k // 512, 128, 2 * n)
    return np.ascontiguousarray(words), np.ascontiguousarray(byte.astype(np.uint8).reshape(k // 512, 16, n))


def unpack_weight(words, scales, fmt):
    g, _, n = scales.shape
    words = np.ascontiguousarray(words).reshape(g, 128, n, -1)
    if fmt == "e4m3":
        vals = words.view(ml_dtypes.float8_e4m3fn).astype(np.float64)
    else:
        nib = np.empty((g, 128, n, 4), np.uint8)
        nib[..., 0::2] = words & 0xF
        nib[..., 1::2] = words >> 4
        vals = E2M1[nib]
    vals = vals * np.repeat(np.exp2(scales.astype(np.float64) - 127.0), 8, axis=1)[..., None]
    return vals.transpose(0, 1, 3, 2).reshape(g * 512, n)


def gelu(v):
    return 0.5 * v * (1.0 + np.tanh(np.sqrt(2.0 / np.pi) * (v + 0.044715 * v**3)))


K, T, S, P, H = 1536, 2048, 1024, 512, 512

def setup_inputs():
    n = np.random.standard_normal
    s = mx_kscale(K)[:, None]
    u = mx_kscale(H)[:, None]
    tab_words, tab_scales = pack_weight(n((K, T)) * s, "e4m3")
    w1_words, w1_scales = pack_weight(1.2 * n((K, H)) / np.sqrt(K) / s, "e2m1")
    return {
        "tab_words": tab_words, "tab_scales": tab_scales,
        "offs": striped(np.random.permutation(T)[:S]),
        "w1_words": w1_words, "w1_scales": w1_scales,
        "w2": (0.52 * n((K, H)) / np.sqrt(K) / s).astype(np.float32),
        "gain": (np.exp(0.3 * n(H)) * u[:, 0]).astype(np.float32),
        "pos1": striped(np.random.permutation(S)[:P]),
        "refm": (n((H, P)) * u).astype(np.float32),
        "w3": (1.3 * n((H, H)) / np.sqrt(H) / u).astype(np.float32),
        "b": (0.5 * n(H)).astype(np.float32),
        "skip": (np.exp(0.3 * n(H)) / u[:, 0]).astype(np.float32),
        "offm": (0.7 * n((H, S))).astype(np.float32),
        "wgo": np.exp(0.3 * n((128, P))).astype(np.float32),
    }

def reference(tab_words, tab_scales, offs, w1_words, w1_scales, w2, gain, pos1, refm, w3, b, skip, offm, wgo):
    v = unpack_weight(tab_words, tab_scales, "e4m3")[:, unstriped(offs)]
    w1 = unpack_weight(w1_words, w1_scales, "e2m1")
    w2q = mxq(f64(w2), 0, "e4m3")
    w3q = mxq(f64(w3), 0, "e4m3")
    level = w1.T @ v
    phase = w2q.T @ v
    h = f64(gain)[:, None] * (level * np.cos(phase))
    x = np.maximum(h[:, unstriped(pos1)], f64(refm))
    xq = mxq(x, 0, "e4m3")
    y = np.tanh((w3q.T @ xq) + f64(b)[:, None])
    out = f64(skip)[:, None] * h + f64(offm)
    out[:, unstriped(pos1)] = np.tile(f64(wgo), (H // 128, 1)) * y
    return out

@@ -1,0 +1,284 @@
+import math
+from contextlib import ExitStack
+
+import concourse.mybir as mybir
+
+K, T, S, M2, H = 1536, 2048, 1024, 512, 512
+FLOPS = 2 * K * H * S * 2 + 2 * H * H * M2
+
+F32 = mybir.dt.float32
+BF16 = mybir.dt.bfloat16
+I32 = mybir.dt.int32
+U32 = mybir.dt.uint32
+U16 = mybir.dt.uint16
+U8 = mybir.dt.uint8
+FP8X4 = mybir.dt.float8_e4m3fn_x4
+FP4X4 = mybir.dt.float4_e2m1fn_x4
+ALU = mybir.AluOpType
+ACT = mybir.ActivationFunctionType
+
+P = 128
+PACK = 4
+PASSES = K // (P * PACK)
+N = 512
+HALVES = S // N
+UNITS = PACK * HALVES
+BANKS = 4
+SHIFT_ROWS = 112
+
+
+def round_and_deal(nc, pool, raw, pair):
+    grouped = pool.tile([P, 2 * P * PACK], BF16, name="grouped", tag="grouped", bufs=4, align_bytes=64)
+    nc.scalar.copy(
+        grouped[:].rearrange("p (t m j) -> p m t j", t=2, j=PACK),
+        raw[:].rearrange("p j (m t) -> p m t j", t=PACK)[:, :, 2 * pair : 2 * pair + 2, :],
+    )
+    return grouped
+
+
+def quantise_pair(nc, grouped, codes, scales, pair):
+    cols = slice(2 * P * pair, 2 * P * (pair + 1))
+    nc.vector.quantize_mx(out=codes[:, cols].bitcast(FP8X4), scales=scales[:, cols], in_=grouped[:])
+
+
+def tile_list_shutterless_block_correction_kernel(
+    tc, tab_words, tab_scales, offs, w1_words, w1_scales, w2, gain, pos1, refm, w3, b, skip, offm, wgo, out
+):
+    nc = tc.nc
+    with ExitStack() as ctx:
+        lists = ctx.enter_context(tc.tile_pool(name="lists", bufs=1))
+        keep = ctx.enter_context(tc.tile_pool(name="keep", bufs=1))
+        ring = ctx.enter_context(tc.tile_pool(name="ring", bufs=3))
+        psum = ctx.enter_context(tc.psum_pool(name="psum", bufs=BANKS))
+
+        offs_sb = lists.tile([P, S // 16], U16, name="offs_sb")
+        pos_sb = lists.tile([P, M2 // 16], U16, name="pos_sb")
+
+        tab_planes = keep.tile([P, T], U8, name="tab_planes", align_bytes=64)
+        nc.gpsimd.memset(tab_planes[:].bitcast(I32), 0)
+        w1_planes_raw = keep.tile([P, PASSES * H], U8, name="w1_planes_raw", align_bytes=64)
+        nc.gpsimd.memset(w1_planes_raw[:].bitcast(I32), 0)
+        moved = [keep.tile([P, S], U8, name="moved%d" % a, align_bytes=64) for a in range(1, PASSES)]
+        for plane in moved:
+            nc.gpsimd.memset(plane[:].bitcast(I32), 0)
+
+        tab_sb = [keep.tile([P, T], I32, name="tab_sb%d" % a, align_bytes=64) for a in range(PASSES)]
+        w2_raw = [keep.tile([P, PACK, H], F32, name="w2_raw%d" % a, align_bytes=64) for a in range(PASSES)]
+
+        def load_table(a):
+            nc.sync.dma_start(tab_sb[a][:], tab_words[a].rearrange("p t i -> p (t i)").bitcast(I32))
+
+        def load_w2(a):
+            nc.sync.dma_start(w2_raw[a][:], w2[512 * a : 512 * (a + 1), :].rearrange("(p j) c -> p j c", j=PACK))
+
+        nc.sync.dma_start(offs_sb[:], offs)
+        load_table(0)
+        for q in range(4):
+            nc.sync.dma_start(
+                tab_planes[32 * q : 32 * q + 4 * PASSES, :].bitcast(I32),
+                tab_scales[:, 4 * q : 4 * q + 4, :].bitcast(I32),
+            )
+        load_w2(0)
+        load_w2(1)
+        w1_raw = keep.tile([P, PASSES, H // 2], I32, name="w1_raw", align_bytes=64)
+        nc.sync.dma_start(w1_raw[:], w1_words.rearrange("a p c -> p a c").bitcast(I32))
+        for q in range(4):
+            nc.sync.dma_start(
+                w1_planes_raw[32 * q : 32 * q + 4, :].bitcast(I32).rearrange("p (a c) -> p a c", a=PASSES),
+                w1_scales[:, 4 * q : 4 * q + 4, :].rearrange("a r c -> r a c").bitcast(I32),
+            )
+        load_table(1)
+        load_w2(2)
+        load_table(2)
+
+        picked_planes = keep.tile([P, S], U8, name="picked_planes", align_bytes=64)
+        picked = [
+            [keep.tile([P, N], U32, name="picked%d_%d" % (a, half), align_bytes=64) for half in range(HALVES)]
+            for a in range(PASSES)
+        ]
+        planes = [picked_planes] + moved
+        w2_codes = keep.tile([P, PASSES, H], U32, name="w2_codes", align_bytes=64)
+        w2_scales = keep.tile([P, PASSES, H], U8, name="w2_scales", align_bytes=64)
+        w1_codes = keep.tile([P, PACK * PASSES * P * 2], U8, name="w1_codes", align_bytes=64)
+        w1_planes = keep.tile([P, PACK * PASSES * P], U8, name="w1_planes", align_bytes=64)
+
+        def gather_table(a):
+            for half in range(HALVES):
+                nc.vector.tensor_copy(
+                    picked[a][half][:], tab_sb[a][:].bitcast(U32).indirect(offs_sb[:, 32 * half : 32 * (half + 1)])
+                )
+
+        def quantise_w2(a):
+            dealt = [round_and_deal(nc, ring, w2_raw[a], pair) for pair in range(2)]
+            for pair in range(2):
+                quantise_pair(nc, dealt[pair], w2_codes[:, a, :], w2_scales[:, a, :], pair)
+
+        gather_table(0)
+        nc.vector.tensor_copy(picked_planes[:], tab_planes[:].indirect(offs_sb[:]))
+        for i, plane in enumerate(moved):
+            first = 4 * (i + 1)
+            nc.sync.dma_start(
+                plane[0:SHIFT_ROWS, :].bitcast(I32), picked_planes[first : first + SHIFT_ROWS, :].bitcast(I32)
+            )
+
+        gain_sb = keep.tile([P, PACK], F32, name="gain_sb")
+        nc.sync.dma_start(gain_sb[:], gain.rearrange("(p t) -> p t", t=PACK))
+        nc.sync.dma_start(pos_sb[:], pos1)
+        skip_sb = keep.tile([P, PACK], F32, name="skip_sb")
+        nc.sync.dma_start(skip_sb[:], skip.rearrange("(p t) -> p t", t=PACK))
+        offm_rows = offm.rearrange("(p t) j -> t p j", t=PACK)
+        out_rows = out.rearrange("(p t) j -> t p j", t=PACK)
+        offm_sb = [keep.tile([P, S], F32, name="offm_sb%d" % t, align_bytes=64) for t in range(PACK)]
+        nc.sync.dma_start(offm_sb[0][:], offm_rows[0])
+        refm_sb = keep.tile([P, PACK, M2], F32, name="refm_sb", align_bytes=64)
+        nc.sync.dma_start(refm_sb[:], refm.rearrange("(p t) m -> p t m", t=PACK))
+        nc.sync.dma_start(offm_sb[1][:], offm_rows[1])
+        w3_raw = keep.tile([P, PACK, H], F32, name="w3_raw", align_bytes=64)
+        nc.sync.dma_start(w3_raw[:], w3.rearrange("(p j) c -> p j c", j=PACK))
+        for t in range(2, PACK):
+            nc.sync.dma_start(offm_sb[t][:], offm_rows[t])
+        b_sb = keep.tile([P, PACK], F32, name="b_sb")
+        nc.sync.dma_start(b_sb[:], b.rearrange("(p t) -> p t", t=PACK))
+        wgo_sb = keep.tile([P, PACK * M2], F32, name="wgo_sb", align_bytes=64)
+        for q in (0, 2, 1, 3):
+            nc.sync.dma_start(wgo_sb[32 * q : 32 * q + 32, :], wgo.rearrange("(r t) m -> r (t m)", t=PACK))
+
+        phase, level = [None] * UNITS, [None] * UNITS
+
+        def phase_pass(u, a):
+            t, half = divmod(u, HALVES)
+            if a == 0:
+                phase[u] = psum.tile([P, N], F32, name="phase", tag="phase")
+            nc.tensor.matmul_mx(
+                out=phase[u][:],
+                lhsT=w2_codes[:, a, P * t : P * (t + 1)].bitcast(FP8X4),
+                lhsT_scale=w2_scales[:, a, P * t : P * (t + 1)],
+                rhs=picked[a][half][:].bitcast(FP8X4),
+                rhs_scale=picked_planes[4 * a : P, N * half : N * (half + 1)],
+                start=(a == 0),
+                stop=(a == PASSES - 1),
+            )
+
+        def level_pass(u, a):
+            t, half = divmod(u, HALVES)
+            if a == 0:
+                level[u] = psum.tile([P, N], F32, name="level", tag="level")
+            col = (t * PASSES + a) * P
+            nc.tensor.matmul_mx(
+                out=level[u][:],
+                lhsT=w1_codes[:, 2 * col : 2 * (col + P)].bitcast(FP4X4),
+                lhsT_scale=w1_planes[:, col : col + P],
+                rhs=picked[a][half][:].bitcast(FP8X4),
+                rhs_scale=planes[a][:, N * half : N * (half + 1)],
+                start=(a == 0),
+                stop=(a == PASSES - 1),
+            )
+
+        quantise_w2(0)
+        for u in range(BANKS):
+            phase_pass(u, 0)
+        nc.vector.tensor_copy(
+            w1_codes[:].bitcast(U16).rearrange("p (t g m) -> p g t m", t=PACK, m=8),
+            w1_raw[:].rearrange("p a c -> p (a c)").bitcast(U16).rearrange("p (g m t) -> p g t m", t=PACK, m=8),
+        )
+        nc.vector.tensor_copy(
+            w1_planes[:].rearrange("p (t g m) -> p g t m", t=PACK, m=16),
+            w1_planes_raw[:].rearrange("p (g m t) -> p g t m", t=PACK, m=16),
+        )
+        for u in range(BANKS):
+            level_pass(u, 0)
+        gather_table(1)
+        quantise_w2(1)
+        for u in range(BANKS):
+            phase_pass(u, 1)
+        quantise_w2(2)
+        gather_table(2)
+
+        w3_codes = keep.tile([P, H], U32, name="w3_codes", align_bytes=64)
+        w3_scales = keep.tile([P, H], U8, name="w3_scales", align_bytes=64)
+        h = [keep.tile([P, S], F32, name="h%d" % t, align_bytes=64) for t in range(PACK)]
+        x_pairs = keep.tile([P, 2, M2 * 2], BF16, name="x_pairs", align_bytes=64)
+        h_picked = [
+            keep.tile([P, 2, M2], F32, name="h_picked", tag="h_picked%d" % pair, align_bytes=64) for pair in range(2)
+        ]
+        base = [None] * PACK
+        turns, whole, cosine = [None] * UNITS, [None] * UNITS, [None] * UNITS
+
+        def base_tile(t, tag):
+            base[t] = keep.tile([P, S], F32, name="base%d" % t, tag=tag, align_bytes=64)
+            nc.vector.scalar_tensor_tensor(
+                base[t][:], h[t][:], skip_sb[:, t : t + 1], offm_sb[t][:], ALU.mult, ALU.add
+            )
+
+        def count_turns(u):
+            for a in range(PASSES - 1 if u < BANKS else 0, PASSES):
+                phase_pass(u, a)
+            turns[u] = ring.tile([P, N], F32, name="turns", tag="turns", align_bytes=64)
+            nc.scalar.activation(turns[u][:], phase[u][:], ACT.Abs, scale=1.0 / (2.0 * math.pi))
+            whole[u] = ring.tile([P, N], U32, name="whole", tag="whole", align_bytes=64)
+            nc.scalar.activation(whole[u][:], turns[u][:], ACT.Copy, bias=0.25)
+
+        def take_cosine(u):
+            for a in range(1 if u < BANKS else 0, PASSES):
+                level_pass(u, a)
+            frac = ring.tile([P, N], F32, name="frac", tag="frac", align_bytes=64)
+            nc.vector.scalar_tensor_tensor(frac[:], turns[u][:], 0.25, whole[u][:].bitcast(I32), ALU.add, ALU.subtract)
+            cosine[u] = ring.tile([P, N], F32, name="cosine", tag="cosine", align_bytes=64)
+            nc.scalar.activation(cosine[u][:], frac[:], ACT.Sin, scale=2.0 * math.pi)
+
+        def finish_features(u):
+            t, half = divmod(u, HALVES)
+            nc.vector.scalar_tensor_tensor(
+                h[t][:, N * half : N * (half + 1)], level[u][:], gain_sb[:, t : t + 1], cosine[u][:], ALU.mult, ALU.mult
+            )
+            if half == HALVES - 1:
+                pair, slot = divmod(t, 2)
+                nc.vector.tensor_copy(h_picked[pair][:, slot, :], h[t][:].indirect(pos_sb[:]))
+                if slot == 1:
+                    nc.vector.tensor_tensor(
+                        x_pairs[:, pair, :].rearrange("p (m s) -> p m s", s=2),
+                        h_picked[pair][:].rearrange("p s m -> p m s"),
+                        refm_sb[:, 2 * pair : 2 * pair + 2, :].rearrange("p s m -> p m s"),
+                        ALU.max,
+                    )
+
+        for step in range(UNITS + 2):
+            if step < UNITS:
+                count_turns(step)
+            if 1 <= step <= UNITS:
+                take_cosine(step - 1)
+            if step >= 2:
+                finish_features(step - 2)
+        for pair in range(2):
+            dealt3 = round_and_deal(nc, ring, w3_raw, pair)
+            quantise_pair(nc, dealt3, w3_codes, w3_scales, pair)
+
+        x_bf = keep.tile([P, M2 * PACK], BF16, name="x_bf", tag="x_bf", align_bytes=64)
+        nc.scalar.copy(
+            x_bf[:].bitcast(F32).rearrange("p (m u) -> p m u", u=2),
+            x_pairs[:].rearrange("p u w -> p (u w)").bitcast(F32).rearrange("p (u m) -> p m u", u=2),
+        )
+        x_codes = keep.tile([P, M2], U32, name="x_codes", align_bytes=64)
+        x_scales = keep.tile([P, M2], U8, name="x_scales", align_bytes=64)
+        nc.vector.quantize_mx(out=x_codes[:].bitcast(FP8X4), scales=x_scales[:], in_=x_bf[:])
+        base_tile(0, "base0")
+        base_tile(1, "base1")
+        base_tile(2, "h_picked1")
+        base_tile(3, "x_bf")
+        for t in range(PACK):
+            acc = psum.tile([P, M2], F32, name="acc", tag="phase")
+            nc.tensor.matmul_mx(
+                out=acc[:],
+                lhsT=w3_codes[:, P * t : P * (t + 1)].bitcast(FP8X4),
+                lhsT_scale=w3_scales[:, P * t : P * (t + 1)],
+                rhs=x_codes[:].bitcast(FP8X4),
+                rhs_scale=x_scales[:],
+                start=True,
+                stop=True,
+            )
+            y = ring.tile([P, M2], F32, name="y", tag="y", bufs=4, align_bytes=64)
+            nc.scalar.activation(y[:], acc[:], ACT.Tanh, bias=b_sb[:, t : t + 1])
+            nc.vector.tensor_tensor(
+                base[t][:].indirect(pos_sb[:]), y[:], wgo_sb[:, M2 * t : M2 * (t + 1)], ALU.mult
+            )
+            nc.sync.dma_start(out_rows[t], base[t][:])

@@ -2,6 +2,7 @@ import math
 from contextlib import ExitStack
 
 import concourse.mybir as mybir
+from concourse.masks import make_identity
 
 K, T, S, M2, H = 1536, 2048, 1024, 512, 512
 FLOPS = 2 * K * H * S * 2 + 2 * H * H * M2
@@ -22,23 +23,27 @@ PACK = 4
 PASSES = K // (P * PACK)
 N = 512
 HALVES = S // N
-UNITS = PACK * HALVES
-BANKS = 4
+TILES = H // P
+UNITS = TILES * HALVES
+SIDES = 2
+WIDE = H // SIDES
+EARLY = 3
+VECTOR_LED = (0, 1)
 SHIFT_ROWS = 112
+UNIT_ORDER = ((0, 0), (1, 0), (0, 1), (1, 1), (2, 0), (2, 1), (3, 0), (3, 1))
+TURN = 1.0 / (2.0 * math.pi)
 
 
-def round_and_deal(nc, pool, raw, pair):
-    grouped = pool.tile([P, 2 * P * PACK], BF16, name="grouped", tag="grouped", bufs=4, align_bytes=64)
-    nc.scalar.copy(
-        grouped[:].rearrange("p (t m j) -> p m t j", t=2, j=PACK),
-        raw[:].rearrange("p j (m t) -> p m t j", t=PACK)[:, :, 2 * pair : 2 * pair + 2, :],
+def bank(u, role):
+    rnd, place = divmod(u, EARLY)
+    return "bank%d_%d" % ((rnd + role) % 2, place)
+
+
+def round_and_interleave(copy, grouped, raw):
+    copy(
+        grouped.rearrange("p (c i j) -> p c j i", i=4, j=PACK),
+        raw.rearrange("p j (c i) -> p c j i", i=4),
     )
-    return grouped
-
-
-def quantise_pair(nc, grouped, codes, scales, pair):
-    cols = slice(2 * P * pair, 2 * P * (pair + 1))
-    nc.vector.quantize_mx(out=codes[:, cols].bitcast(FP8X4), scales=scales[:, cols], in_=grouped[:])
 
 
 def tile_list_shutterless_block_correction_kernel(
@@ -48,48 +53,69 @@ def tile_list_shutterless_block_correction_kernel(
     with ExitStack() as ctx:
         lists = ctx.enter_context(tc.tile_pool(name="lists", bufs=1))
         keep = ctx.enter_context(tc.tile_pool(name="keep", bufs=1))
-        ring = ctx.enter_context(tc.tile_pool(name="ring", bufs=3))
-        psum = ctx.enter_context(tc.psum_pool(name="psum", bufs=BANKS))
+        ring = ctx.enter_context(tc.tile_pool(name="ring", bufs=2))
+        psum = ctx.enter_context(tc.psum_pool(name="psum", bufs=1))
 
         offs_sb = lists.tile([P, S // 16], U16, name="offs_sb")
         pos_sb = lists.tile([P, M2 // 16], U16, name="pos_sb")
 
         tab_planes = keep.tile([P, T], U8, name="tab_planes", align_bytes=64)
-        nc.gpsimd.memset(tab_planes[:].bitcast(I32), 0)
-        w1_planes_raw = keep.tile([P, PASSES * H], U8, name="w1_planes_raw", align_bytes=64)
-        nc.gpsimd.memset(w1_planes_raw[:].bitcast(I32), 0)
+        nc.vector.memset(tab_planes[:].bitcast(I32), 0)
+        warm = keep.tile([P, 2], F32, name="warm")
+        nc.vector.memset(warm[:, 0:1], 0.0)
+        nc.scalar.activation(warm[:, 1:2], warm[:, 0:1], ACT.Silu)
+        w1_planes = keep.tile([P, PASSES * H], U8, name="w1_planes", align_bytes=64)
+        nc.vector.memset(w1_planes[:].bitcast(I32), 0)
+        for q in range(4):
+            nc.gpsimd.dma_start(
+                w1_planes[32 * q : 32 * q + 4, :].bitcast(I32).rearrange("p (a c) -> p a c", a=PASSES),
+                w1_scales[:, 4 * q : 4 * q + 4, :].rearrange("a r c -> r a c").bitcast(I32),
+            )
         moved = [keep.tile([P, S], U8, name="moved%d" % a, align_bytes=64) for a in range(1, PASSES)]
         for plane in moved:
-            nc.gpsimd.memset(plane[:].bitcast(I32), 0)
+            nc.vector.memset(plane[:].bitcast(I32), 0)
+        vec_rows = keep.tile([P, P], F32, name="vec_rows")
+        nc.vector.memset(vec_rows[:], 0.0)
+        for i, vec in enumerate((gain, skip, b)):
+            nc.gpsimd.dma_start(vec_rows[TILES * i : TILES * (i + 1), :], vec.rearrange("(t p) -> t p", p=P))
+        ident_f32 = keep.tile([P, P], F32, name="ident_f32")
+        make_identity(nc, ident_f32[:])
+        ident_bf16 = keep.tile([P, P], BF16, name="ident_bf16")
+        make_identity(nc, ident_bf16[:])
 
         tab_sb = [keep.tile([P, T], I32, name="tab_sb%d" % a, align_bytes=64) for a in range(PASSES)]
-        w2_raw = [keep.tile([P, PACK, H], F32, name="w2_raw%d" % a, align_bytes=64) for a in range(PASSES)]
+        w2_raw = [
+            [keep.tile([P, PACK, WIDE], F32, name="w2_raw", tag="w2_raw%d_%d" % (side, a), align_bytes=64) for a in range(PASSES)]
+            for side in range(SIDES)
+        ]
 
         def load_table(a):
             nc.sync.dma_start(tab_sb[a][:], tab_words[a].rearrange("p t i -> p (t i)").bitcast(I32))
 
-        def load_w2(a):
-            nc.sync.dma_start(w2_raw[a][:], w2[512 * a : 512 * (a + 1), :].rearrange("(p j) c -> p j c", j=PACK))
+        def load_w2(side, a):
+            nc.sync.dma_start(
+                w2_raw[side][a][:],
+                w2[512 * a : 512 * (a + 1), WIDE * side : WIDE * (side + 1)].rearrange("(p j) c -> p j c", j=PACK),
+            )
 
         nc.sync.dma_start(offs_sb[:], offs)
         load_table(0)
+        load_w2(0, 0)
         for q in range(4):
             nc.sync.dma_start(
                 tab_planes[32 * q : 32 * q + 4 * PASSES, :].bitcast(I32),
                 tab_scales[:, 4 * q : 4 * q + 4, :].bitcast(I32),
             )
-        load_w2(0)
-        load_w2(1)
-        w1_raw = keep.tile([P, PASSES, H // 2], I32, name="w1_raw", align_bytes=64)
-        nc.sync.dma_start(w1_raw[:], w1_words.rearrange("a p c -> p a c").bitcast(I32))
-        for q in range(4):
-            nc.sync.dma_start(
-                w1_planes_raw[32 * q : 32 * q + 4, :].bitcast(I32).rearrange("p (a c) -> p a c", a=PASSES),
-                w1_scales[:, 4 * q : 4 * q + 4, :].rearrange("a r c -> r a c").bitcast(I32),
-            )
         load_table(1)
-        load_w2(2)
+        load_w2(0, 1)
+        load_w2(0, 2)
         load_table(2)
+        load_w2(1, 0)
+        w1_codes = keep.tile([P, PASSES * 2 * H], U8, name="w1_codes", align_bytes=64)
+        nc.sync.dma_start(
+            w1_codes[:].bitcast(I32).rearrange("p (a c) -> p a c", a=PASSES),
+            w1_words.rearrange("a p c -> p a c").bitcast(I32),
+        )
 
         picked_planes = keep.tile([P, S], U8, name="picked_planes", align_bytes=64)
         picked = [
@@ -97,23 +123,27 @@ def tile_list_shutterless_block_correction_kernel(
             for a in range(PASSES)
         ]
         planes = [picked_planes] + moved
-        w2_codes = keep.tile([P, PASSES, H], U32, name="w2_codes", align_bytes=64)
-        w2_scales = keep.tile([P, PASSES, H], U8, name="w2_scales", align_bytes=64)
-        w1_codes = keep.tile([P, PACK * PASSES * P * 2], U8, name="w1_codes", align_bytes=64)
-        w1_planes = keep.tile([P, PACK * PASSES * P], U8, name="w1_planes", align_bytes=64)
+        w2_codes = [
+            [keep.tile([P, WIDE], U32, name="w2_codes%d_%d" % (side, a), align_bytes=64) for a in range(PASSES)]
+            for side in range(SIDES)
+        ]
+        w2_scales = [
+            [keep.tile([P, WIDE], U8, name="w2_scales%d_%d" % (side, a), align_bytes=64) for a in range(PASSES)]
+            for side in range(SIDES)
+        ]
 
-        def gather_table(a):
-            for half in range(HALVES):
-                nc.vector.tensor_copy(
-                    picked[a][half][:], tab_sb[a][:].bitcast(U32).indirect(offs_sb[:, 32 * half : 32 * (half + 1)])
-                )
+        def gather_table(a, half):
+            nc.vector.tensor_copy(
+                picked[a][half][:], tab_sb[a][:].bitcast(U32).indirect(offs_sb[:, 32 * half : 32 * (half + 1)])
+            )
 
-        def quantise_w2(a):
-            dealt = [round_and_deal(nc, ring, w2_raw[a], pair) for pair in range(2)]
-            for pair in range(2):
-                quantise_pair(nc, dealt[pair], w2_codes[:, a, :], w2_scales[:, a, :], pair)
+        def quantise_w2(side, a, copy=nc.scalar.copy, tag=None):
+            grouped = keep.tile([P, WIDE * PACK], BF16, name="grouped", tag=tag or "grouped%d_%d" % (side, a), align_bytes=64)
+            round_and_interleave(copy, grouped[:], w2_raw[side][a][:])
+            nc.vector.quantize_mx(out=w2_codes[side][a][:].bitcast(FP8X4), scales=w2_scales[side][a][:], in_=grouped[:])
 
-        gather_table(0)
+        for half in range(HALVES):
+            gather_table(0, half)
         nc.vector.tensor_copy(picked_planes[:], tab_planes[:].indirect(offs_sb[:]))
         for i, plane in enumerate(moved):
             first = 4 * (i + 1)
@@ -121,38 +151,32 @@ def tile_list_shutterless_block_correction_kernel(
                 plane[0:SHIFT_ROWS, :].bitcast(I32), picked_planes[first : first + SHIFT_ROWS, :].bitcast(I32)
             )
 
-        gain_sb = keep.tile([P, PACK], F32, name="gain_sb")
-        nc.sync.dma_start(gain_sb[:], gain.rearrange("(p t) -> p t", t=PACK))
         nc.sync.dma_start(pos_sb[:], pos1)
-        skip_sb = keep.tile([P, PACK], F32, name="skip_sb")
-        nc.sync.dma_start(skip_sb[:], skip.rearrange("(p t) -> p t", t=PACK))
-        offm_rows = offm.rearrange("(p t) j -> t p j", t=PACK)
-        out_rows = out.rearrange("(p t) j -> t p j", t=PACK)
-        offm_sb = [keep.tile([P, S], F32, name="offm_sb%d" % t, align_bytes=64) for t in range(PACK)]
-        nc.sync.dma_start(offm_sb[0][:], offm_rows[0])
-        refm_sb = keep.tile([P, PACK, M2], F32, name="refm_sb", align_bytes=64)
-        nc.sync.dma_start(refm_sb[:], refm.rearrange("(p t) m -> p t m", t=PACK))
-        nc.sync.dma_start(offm_sb[1][:], offm_rows[1])
+        refm_sb = [keep.tile([P, M2], F32, name="refm_sb", tag="refm%d" % t, align_bytes=64) for t in range(TILES)]
+        offm_sb = [keep.tile([P, S], F32, name="offm_sb%d" % t, align_bytes=64) for t in range(TILES)]
+        load_w2(1, 1)
+        load_w2(1, 2)
+        for t in range(TILES):
+            nc.sync.dma_start(refm_sb[t][:], refm[P * t : P * (t + 1), :])
         w3_raw = keep.tile([P, PACK, H], F32, name="w3_raw", align_bytes=64)
         nc.sync.dma_start(w3_raw[:], w3.rearrange("(p j) c -> p j c", j=PACK))
-        for t in range(2, PACK):
-            nc.sync.dma_start(offm_sb[t][:], offm_rows[t])
-        b_sb = keep.tile([P, PACK], F32, name="b_sb")
-        nc.sync.dma_start(b_sb[:], b.rearrange("(p t) -> p t", t=PACK))
-        wgo_sb = keep.tile([P, PACK * M2], F32, name="wgo_sb", align_bytes=64)
-        for q in (0, 2, 1, 3):
-            nc.sync.dma_start(wgo_sb[32 * q : 32 * q + 32, :], wgo.rearrange("(r t) m -> r (t m)", t=PACK))
+        for t in range(TILES):
+            nc.sync.dma_start(offm_sb[t][:], offm[P * t : P * (t + 1), :])
+        wgo_sb = keep.tile([P, M2], F32, name="wgo_sb", align_bytes=64)
+        nc.sync.dma_start(wgo_sb[:], wgo)
 
         phase, level = [None] * UNITS, [None] * UNITS
 
         def phase_pass(u, a):
-            t, half = divmod(u, HALVES)
+            t, half = UNIT_ORDER[u]
+            side, place = divmod(t, TILES // SIDES)
+            cols = slice(P * place, P * (place + 1))
             if a == 0:
-                phase[u] = psum.tile([P, N], F32, name="phase", tag="phase")
+                phase[u] = psum.tile([P, N], F32, name="phase", tag=bank(u, 0))
             nc.tensor.matmul_mx(
                 out=phase[u][:],
-                lhsT=w2_codes[:, a, P * t : P * (t + 1)].bitcast(FP8X4),
-                lhsT_scale=w2_scales[:, a, P * t : P * (t + 1)],
+                lhsT=w2_codes[side][a][:, cols].bitcast(FP8X4),
+                lhsT_scale=w2_scales[side][a][:, cols],
                 rhs=picked[a][half][:].bitcast(FP8X4),
                 rhs_scale=picked_planes[4 * a : P, N * half : N * (half + 1)],
                 start=(a == 0),
@@ -160,10 +184,10 @@ def tile_list_shutterless_block_correction_kernel(
             )
 
         def level_pass(u, a):
-            t, half = divmod(u, HALVES)
+            t, half = UNIT_ORDER[u]
             if a == 0:
-                level[u] = psum.tile([P, N], F32, name="level", tag="level")
-            col = (t * PASSES + a) * P
+                level[u] = psum.tile([P, N], F32, name="level", tag=bank(u, 1))
+            col = H * a + P * t
             nc.tensor.matmul_mx(
                 out=level[u][:],
                 lhsT=w1_codes[:, 2 * col : 2 * (col + P)].bitcast(FP4X4),
@@ -174,73 +198,87 @@ def tile_list_shutterless_block_correction_kernel(
                 stop=(a == PASSES - 1),
             )
 
-        quantise_w2(0)
-        for u in range(BANKS):
-            phase_pass(u, 0)
-        nc.vector.tensor_copy(
-            w1_codes[:].bitcast(U16).rearrange("p (t g m) -> p g t m", t=PACK, m=8),
-            w1_raw[:].rearrange("p a c -> p (a c)").bitcast(U16).rearrange("p (g m t) -> p g t m", t=PACK, m=8),
-        )
-        nc.vector.tensor_copy(
-            w1_planes[:].rearrange("p (t g m) -> p g t m", t=PACK, m=16),
-            w1_planes_raw[:].rearrange("p (g m t) -> p g t m", t=PACK, m=16),
-        )
-        for u in range(BANKS):
-            level_pass(u, 0)
-        gather_table(1)
-        quantise_w2(1)
-        for u in range(BANKS):
-            phase_pass(u, 1)
-        quantise_w2(2)
-        gather_table(2)
+        for a in range(PASSES):
+            if a == 1:
+                for half in range(HALVES):
+                    gather_table(a, half)
+            quantise_w2(0, a)
+            if a < PASSES - 1:
+                for u in range(EARLY):
+                    phase_pass(u, a)
+        for half in range(HALVES):
+            gather_table(PASSES - 1, half)
+        quantise_w2(1, 0)
+
+        vec_turned = psum.tile([P, P], F32, name="vec_turned", tag="turn", bufs=2)
+        nc.tensor.transpose(vec_turned[:], vec_rows[:], ident_f32[:])
+        vec_cols = keep.tile([P, 3 * TILES], F32, name="vec_cols")
+        nc.scalar.copy(vec_cols[:], vec_turned[:, 0 : 3 * TILES])
 
         w3_codes = keep.tile([P, H], U32, name="w3_codes", align_bytes=64)
         w3_scales = keep.tile([P, H], U8, name="w3_scales", align_bytes=64)
-        h = [keep.tile([P, S], F32, name="h%d" % t, align_bytes=64) for t in range(PACK)]
-        x_pairs = keep.tile([P, 2, M2 * 2], BF16, name="x_pairs", align_bytes=64)
-        h_picked = [
-            keep.tile([P, 2, M2], F32, name="h_picked", tag="h_picked%d" % pair, align_bytes=64) for pair in range(2)
-        ]
-        base = [None] * PACK
+        h = [keep.tile([P, S], F32, name="h%d" % t, align_bytes=64) for t in range(TILES)]
+        x_turned = keep.tile([P, M2 // P, 2, P], F32, name="x_turned", tag="x_turned", align_bytes=64)
         turns, whole, cosine = [None] * UNITS, [None] * UNITS, [None] * UNITS
-
-        def base_tile(t, tag):
-            base[t] = keep.tile([P, S], F32, name="base%d" % t, tag=tag, align_bytes=64)
-            nc.vector.scalar_tensor_tensor(
-                base[t][:], h[t][:], skip_sb[:, t : t + 1], offm_sb[t][:], ALU.mult, ALU.add
-            )
+        x_tiles, picked_tiles = [], []
 
         def count_turns(u):
-            for a in range(PASSES - 1 if u < BANKS else 0, PASSES):
+            for a in range(PASSES - 1 if u < EARLY else 0, PASSES):
                 phase_pass(u, a)
-            turns[u] = ring.tile([P, N], F32, name="turns", tag="turns", align_bytes=64)
-            nc.scalar.activation(turns[u][:], phase[u][:], ACT.Abs, scale=1.0 / (2.0 * math.pi))
-            whole[u] = ring.tile([P, N], U32, name="whole", tag="whole", align_bytes=64)
+            if u in VECTOR_LED:
+                whole[u] = ring.tile([P, N], I32, name="whole_signed", tag="whole_signed", align_bytes=64)
+                nc.vector.tensor_scalar(whole[u][:], phase[u][:], TURN, 0.25, ALU.mult, ALU.add)
+                return
+            if u == len(VECTOR_LED):
+                turns[u] = keep.tile([P, N], F32, name="turns", tag="w2_raw1_0", align_bytes=64)
+            else:
+                turns[u] = ring.tile([P, N], F32, name="turns", tag="turns", bufs=3, align_bytes=64)
+            nc.scalar.activation(turns[u][:], phase[u][:], ACT.Abs, scale=TURN)
+            whole[u] = ring.tile([P, N], U32, name="whole", tag="whole", bufs=3, align_bytes=64)
             nc.scalar.activation(whole[u][:], turns[u][:], ACT.Copy, bias=0.25)
 
         def take_cosine(u):
-            for a in range(1 if u < BANKS else 0, PASSES):
+            for a in range(PASSES):
                 level_pass(u, a)
-            frac = ring.tile([P, N], F32, name="frac", tag="frac", align_bytes=64)
-            nc.vector.scalar_tensor_tensor(frac[:], turns[u][:], 0.25, whole[u][:].bitcast(I32), ALU.add, ALU.subtract)
-            cosine[u] = ring.tile([P, N], F32, name="cosine", tag="cosine", align_bytes=64)
-            nc.scalar.activation(cosine[u][:], frac[:], ACT.Sin, scale=2.0 * math.pi)
+            frac = keep.tile([P, N], F32, name="frac", tag="frac%d" % u, align_bytes=64)
+            if u in (0, UNITS - 1):
+                cosine[u] = keep.tile([P, N], F32, name="cosine", tag="cosine%d" % u, align_bytes=64)
+            else:
+                cosine[u] = ring.tile([P, N], F32, name="cosine", tag="cosine", align_bytes=64)
+            if u in VECTOR_LED:
+                nc.vector.scalar_tensor_tensor(frac[:], phase[u][:], TURN, whole[u][:], ALU.mult, ALU.subtract)
+                nc.scalar.activation(cosine[u][:], frac[:], ACT.Sin, scale=2.0 * math.pi, bias=math.pi / 2.0)
+            else:
+                nc.vector.scalar_tensor_tensor(
+                    frac[:], turns[u][:], 0.25, whole[u][:].bitcast(I32), ALU.add, ALU.subtract
+                )
+                nc.scalar.activation(cosine[u][:], frac[:], ACT.Sin, scale=2.0 * math.pi)
 
         def finish_features(u):
-            t, half = divmod(u, HALVES)
+            t, half = UNIT_ORDER[u]
             nc.vector.scalar_tensor_tensor(
-                h[t][:, N * half : N * (half + 1)], level[u][:], gain_sb[:, t : t + 1], cosine[u][:], ALU.mult, ALU.mult
+                h[t][:, N * half : N * (half + 1)], level[u][:], vec_cols[:, t : t + 1], cosine[u][:], ALU.mult, ALU.mult
             )
-            if half == HALVES - 1:
-                pair, slot = divmod(t, 2)
-                nc.vector.tensor_copy(h_picked[pair][:, slot, :], h[t][:].indirect(pos_sb[:]))
-                if slot == 1:
-                    nc.vector.tensor_tensor(
-                        x_pairs[:, pair, :].rearrange("p (m s) -> p m s", s=2),
-                        h_picked[pair][:].rearrange("p s m -> p m s"),
-                        refm_sb[:, 2 * pair : 2 * pair + 2, :].rearrange("p s m -> p m s"),
-                        ALU.max,
-                    )
+
+        def pick_columns(t, tag):
+            h_picked = keep.tile([P, M2], F32, name="h_picked", tag=tag, align_bytes=64)
+            nc.vector.tensor_copy(h_picked[:], h[t][:].indirect(pos_sb[:]))
+            picked_tiles.append(h_picked)
+
+        def take_maximum(t, tag):
+            x_rows = keep.tile([P, M2], BF16, name="x_rows", tag=tag, align_bytes=64)
+            nc.vector.tensor_tensor(x_rows[:], picked_tiles[t][:], refm_sb[t][:], ALU.max)
+            x_tiles.append(x_rows)
+
+        def turn_rows(t, tag, bufs):
+            turned = psum.tile([P, M2], BF16, name="turned", tag=tag, bufs=bufs)
+            for blk in range(M2 // P):
+                cols = slice(P * blk, P * (blk + 1))
+                nc.tensor.transpose(turned[:, cols], x_tiles[t][:, cols], ident_bf16[:])
+            nc.scalar.copy(
+                x_turned[:, :, :, 32 * t : 32 * (t + 1)],
+                turned[:].bitcast(F32).rearrange("m (blk p u) -> m blk u p", blk=M2 // P, u=2),
+            )
 
         for step in range(UNITS + 2):
             if step < UNITS:
@@ -249,24 +287,56 @@ def tile_list_shutterless_block_correction_kernel(
                 take_cosine(step - 1)
             if step >= 2:
                 finish_features(step - 2)
-        for pair in range(2):
-            dealt3 = round_and_deal(nc, ring, w3_raw, pair)
-            quantise_pair(nc, dealt3, w3_codes, w3_scales, pair)
+            if step == 3:
+                quantise_w2(1, 2, copy=nc.vector.tensor_copy, tag="cosine0")
+                quantise_w2(1, 1, tag="frac2")
+            if step == 4:
+                pick_columns(0, "h_picked0")
+                take_maximum(0, "x_rows0")
+            if step == 5:
+                pick_columns(1, "h_picked1")
+                take_maximum(1, "x_rows1")
+            if step == 8:
+                pick_columns(2, "frac6")
+            if step == 9:
+                take_maximum(2, "frac7")
 
-        x_bf = keep.tile([P, M2 * PACK], BF16, name="x_bf", tag="x_bf", align_bytes=64)
-        nc.scalar.copy(
-            x_bf[:].bitcast(F32).rearrange("p (m u) -> p m u", u=2),
-            x_pairs[:].rearrange("p u w -> p (u w)").bitcast(F32).rearrange("p (u m) -> p m u", u=2),
-        )
+        pick_columns(TILES - 1, "h_picked_last")
+        take_maximum(TILES - 1, "x_rows_last")
+        for t in range(TILES - 1):
+            turn_rows(t, bank(UNITS - 3 + t, 0), 1)
+        grouped3 = keep.tile([P, H * PACK], BF16, name="grouped3", tag="cosine%d" % (UNITS - 1), align_bytes=64)
+        round_and_interleave(nc.scalar.copy, grouped3[:], w3_raw[:])
+        nc.vector.quantize_mx(out=w3_codes[:].bitcast(FP8X4), scales=w3_scales[:], in_=grouped3[:])
+
+        turn_rows(TILES - 1, "turn", 2)
         x_codes = keep.tile([P, M2], U32, name="x_codes", align_bytes=64)
         x_scales = keep.tile([P, M2], U8, name="x_scales", align_bytes=64)
-        nc.vector.quantize_mx(out=x_codes[:].bitcast(FP8X4), scales=x_scales[:], in_=x_bf[:])
-        base_tile(0, "base0")
-        base_tile(1, "base1")
-        base_tile(2, "h_picked1")
-        base_tile(3, "x_bf")
-        for t in range(PACK):
-            acc = psum.tile([P, M2], F32, name="acc", tag="phase")
+        for c in range(2):
+            back = psum.tile([P, 2, 2, P], F32, name="back", tag="turn", bufs=2)
+            for blk in range(2):
+                for u in range(2):
+                    nc.tensor.transpose(back[:, blk, u, :], x_turned[:, 2 * c + blk, u, :], ident_f32[:])
+            x_words = keep.tile([P, M2], F32, name="x_words", tag="x_words%d" % c, align_bytes=64)
+            nc.scalar.copy(
+                x_words[:].rearrange("p (blk m u) -> p blk m u", blk=2, u=2),
+                back[:].rearrange("p blk u m -> p blk m u"),
+            )
+            cols = slice(M2 // 2 * c, M2 // 2 * (c + 1))
+            nc.vector.quantize_mx(
+                out=x_codes[:, cols].bitcast(FP8X4), scales=x_scales[:, cols], in_=x_words[:].bitcast(BF16)
+            )
+
+        base = []
+        last = TILES - 1
+        for t, tag in enumerate(("h_picked_last", "refm%d" % last, "x_rows_last", "x_words1")):
+            page = keep.tile([P, S], F32, name="base%d" % t, tag=tag, align_bytes=64)
+            nc.vector.scalar_tensor_tensor(
+                page[:], h[t][:], vec_cols[:, TILES + t : TILES + t + 1], offm_sb[t][:], ALU.mult, ALU.add
+            )
+            base.append(page)
+        for t in range(TILES):
+            acc = psum.tile([P, M2], F32, name="acc", tag=bank(UNITS - 4 + t, 1))
             nc.tensor.matmul_mx(
                 out=acc[:],
                 lhsT=w3_codes[:, P * t : P * (t + 1)].bitcast(FP8X4),
@@ -277,8 +347,6 @@ def tile_list_shutterless_block_correction_kernel(
                 stop=True,
             )
             y = ring.tile([P, M2], F32, name="y", tag="y", bufs=4, align_bytes=64)
-            nc.scalar.activation(y[:], acc[:], ACT.Tanh, bias=b_sb[:, t : t + 1])
-            nc.vector.tensor_tensor(
-                base[t][:].indirect(pos_sb[:]), y[:], wgo_sb[:, M2 * t : M2 * (t + 1)], ALU.mult
-            )
-            nc.sync.dma_start(out_rows[t], base[t][:])
+            nc.scalar.activation(y[:], acc[:], ACT.Tanh, bias=vec_cols[:, 2 * TILES + t : 2 * TILES + t + 1])
+            nc.vector.tensor_tensor(base[t][:].indirect(pos_sb[:]), y[:], wgo_sb[:], ALU.mult)
+            nc.sync.dma_start(out[P * t : P * (t + 1), :], base[t][:])

import math
from contextlib import ExitStack

import concourse.mybir as mybir
from concourse.masks import make_identity

K, T, S, M2, H = 1536, 2048, 1024, 512, 512
FLOPS = 2 * K * H * S * 2 + 2 * H * H * M2

F32 = mybir.dt.float32
BF16 = mybir.dt.bfloat16
I32 = mybir.dt.int32
U32 = mybir.dt.uint32
U16 = mybir.dt.uint16
U8 = mybir.dt.uint8
FP8X4 = mybir.dt.float8_e4m3fn_x4
FP4X4 = mybir.dt.float4_e2m1fn_x4
ALU = mybir.AluOpType
ACT = mybir.ActivationFunctionType

P = 128
PACK = 4
PASSES = K // (P * PACK)
N = 512
HALVES = S // N
TILES = H // P
UNITS = TILES * HALVES
SIDES = 2
WIDE = H // SIDES
EARLY = 3
VECTOR_LED = (0, 1)
SHIFT_ROWS = 112
UNIT_ORDER = ((0, 0), (1, 0), (0, 1), (1, 1), (2, 0), (2, 1), (3, 0), (3, 1))
TURN = 1.0 / (2.0 * math.pi)


def bank(u, role):
    rnd, place = divmod(u, EARLY)
    return "bank%d_%d" % ((rnd + role) % 2, place)


def round_and_interleave(copy, grouped, raw):
    copy(
        grouped.rearrange("p (c i j) -> p c j i", i=4, j=PACK),
        raw.rearrange("p j (c i) -> p c j i", i=4),
    )


def tile_list_shutterless_block_correction_kernel(
    tc, tab_words, tab_scales, offs, w1_words, w1_scales, w2, gain, pos1, refm, w3, b, skip, offm, wgo, out
):
    nc = tc.nc
    with ExitStack() as ctx:
        lists = ctx.enter_context(tc.tile_pool(name="lists", bufs=1))
        keep = ctx.enter_context(tc.tile_pool(name="keep", bufs=1))
        ring = ctx.enter_context(tc.tile_pool(name="ring", bufs=2))
        psum = ctx.enter_context(tc.psum_pool(name="psum", bufs=1))

        offs_sb = lists.tile([P, S // 16], U16, name="offs_sb")
        pos_sb = lists.tile([P, M2 // 16], U16, name="pos_sb")

        tab_planes = keep.tile([P, T], U8, name="tab_planes", align_bytes=64)
        nc.vector.memset(tab_planes[:].bitcast(I32), 0)
        warm = keep.tile([P, 2], F32, name="warm")
        nc.vector.memset(warm[:, 0:1], 0.0)
        nc.scalar.activation(warm[:, 1:2], warm[:, 0:1], ACT.Silu)
        w1_planes = keep.tile([P, PASSES * H], U8, name="w1_planes", align_bytes=64)
        nc.vector.memset(w1_planes[:].bitcast(I32), 0)
        for q in range(4):
            nc.gpsimd.dma_start(
                w1_planes[32 * q : 32 * q + 4, :].bitcast(I32).rearrange("p (a c) -> p a c", a=PASSES),
                w1_scales[:, 4 * q : 4 * q + 4, :].rearrange("a r c -> r a c").bitcast(I32),
            )
        moved = [keep.tile([P, S], U8, name="moved%d" % a, align_bytes=64) for a in range(1, PASSES)]
        for plane in moved:
            nc.vector.memset(plane[:].bitcast(I32), 0)
        vec_rows = keep.tile([P, P], F32, name="vec_rows")
        nc.vector.memset(vec_rows[:], 0.0)
        for i, vec in enumerate((gain, skip, b)):
            nc.gpsimd.dma_start(vec_rows[TILES * i : TILES * (i + 1), :], vec.rearrange("(t p) -> t p", p=P))
        ident_f32 = keep.tile([P, P], F32, name="ident_f32")
        make_identity(nc, ident_f32[:])
        ident_bf16 = keep.tile([P, P], BF16, name="ident_bf16")
        make_identity(nc, ident_bf16[:])

        tab_sb = [keep.tile([P, T], I32, name="tab_sb%d" % a, align_bytes=64) for a in range(PASSES)]
        w2_raw = [
            [keep.tile([P, PACK, WIDE], F32, name="w2_raw", tag="w2_raw%d_%d" % (side, a), align_bytes=64) for a in range(PASSES)]
            for side in range(SIDES)
        ]

        def load_table(a):
            nc.sync.dma_start(tab_sb[a][:], tab_words[a].rearrange("p t i -> p (t i)").bitcast(I32))

        def load_w2(side, a):
            nc.sync.dma_start(
                w2_raw[side][a][:],
                w2[512 * a : 512 * (a + 1), WIDE * side : WIDE * (side + 1)].rearrange("(p j) c -> p j c", j=PACK),
            )

        nc.sync.dma_start(offs_sb[:], offs)
        load_table(0)
        load_w2(0, 0)
        for q in range(4):
            nc.sync.dma_start(
                tab_planes[32 * q : 32 * q + 4 * PASSES, :].bitcast(I32),
                tab_scales[:, 4 * q : 4 * q + 4, :].bitcast(I32),
            )
        load_table(1)
        load_w2(0, 1)
        load_w2(0, 2)
        load_table(2)
        load_w2(1, 0)
        w1_codes = keep.tile([P, PASSES * 2 * H], U8, name="w1_codes", align_bytes=64)
        nc.sync.dma_start(
            w1_codes[:].bitcast(I32).rearrange("p (a c) -> p a c", a=PASSES),
            w1_words.rearrange("a p c -> p a c").bitcast(I32),
        )

        picked_planes = keep.tile([P, S], U8, name="picked_planes", align_bytes=64)
        picked = [
            [keep.tile([P, N], U32, name="picked%d_%d" % (a, half), align_bytes=64) for half in range(HALVES)]
            for a in range(PASSES)
        ]
        planes = [picked_planes] + moved
        w2_codes = [
            [keep.tile([P, WIDE], U32, name="w2_codes%d_%d" % (side, a), align_bytes=64) for a in range(PASSES)]
            for side in range(SIDES)
        ]
        w2_scales = [
            [keep.tile([P, WIDE], U8, name="w2_scales%d_%d" % (side, a), align_bytes=64) for a in range(PASSES)]
            for side in range(SIDES)
        ]

        def gather_table(a, half):
            nc.vector.tensor_copy(
                picked[a][half][:], tab_sb[a][:].bitcast(U32).indirect(offs_sb[:, 32 * half : 32 * (half + 1)])
            )

        def quantise_w2(side, a, copy=nc.scalar.copy, tag=None):
            grouped = keep.tile([P, WIDE * PACK], BF16, name="grouped", tag=tag or "grouped%d_%d" % (side, a), align_bytes=64)
            round_and_interleave(copy, grouped[:], w2_raw[side][a][:])
            nc.vector.quantize_mx(out=w2_codes[side][a][:].bitcast(FP8X4), scales=w2_scales[side][a][:], in_=grouped[:])

        for half in range(HALVES):
            gather_table(0, half)
        nc.vector.tensor_copy(picked_planes[:], tab_planes[:].indirect(offs_sb[:]))
        for i, plane in enumerate(moved):
            first = 4 * (i + 1)
            nc.sync.dma_start(
                plane[0:SHIFT_ROWS, :].bitcast(I32), picked_planes[first : first + SHIFT_ROWS, :].bitcast(I32)
            )

        nc.sync.dma_start(pos_sb[:], pos1)
        refm_sb = [keep.tile([P, M2], F32, name="refm_sb", tag="refm%d" % t, align_bytes=64) for t in range(TILES)]
        offm_sb = [keep.tile([P, S], F32, name="offm_sb%d" % t, align_bytes=64) for t in range(TILES)]
        load_w2(1, 1)
        load_w2(1, 2)
        for t in range(TILES):
            nc.sync.dma_start(refm_sb[t][:], refm[P * t : P * (t + 1), :])
        w3_raw = keep.tile([P, PACK, H], F32, name="w3_raw", align_bytes=64)
        nc.sync.dma_start(w3_raw[:], w3.rearrange("(p j) c -> p j c", j=PACK))
        for t in range(TILES):
            nc.sync.dma_start(offm_sb[t][:], offm[P * t : P * (t + 1), :])
        wgo_sb = keep.tile([P, M2], F32, name="wgo_sb", align_bytes=64)
        nc.sync.dma_start(wgo_sb[:], wgo)

        phase, level = [None] * UNITS, [None] * UNITS

        def phase_pass(u, a):
            t, half = UNIT_ORDER[u]
            side, place = divmod(t, TILES // SIDES)
            cols = slice(P * place, P * (place + 1))
            if a == 0:
                phase[u] = psum.tile([P, N], F32, name="phase", tag=bank(u, 0))
            nc.tensor.matmul_mx(
                out=phase[u][:],
                lhsT=w2_codes[side][a][:, cols].bitcast(FP8X4),
                lhsT_scale=w2_scales[side][a][:, cols],
                rhs=picked[a][half][:].bitcast(FP8X4),
                rhs_scale=picked_planes[4 * a : P, N * half : N * (half + 1)],
                start=(a == 0),
                stop=(a == PASSES - 1),
            )

        def level_pass(u, a):
            t, half = UNIT_ORDER[u]
            if a == 0:
                level[u] = psum.tile([P, N], F32, name="level", tag=bank(u, 1))
            col = H * a + P * t
            nc.tensor.matmul_mx(
                out=level[u][:],
                lhsT=w1_codes[:, 2 * col : 2 * (col + P)].bitcast(FP4X4),
                lhsT_scale=w1_planes[:, col : col + P],
                rhs=picked[a][half][:].bitcast(FP8X4),
                rhs_scale=planes[a][:, N * half : N * (half + 1)],
                start=(a == 0),
                stop=(a == PASSES - 1),
            )

        for a in range(PASSES):
            if a == 1:
                for half in range(HALVES):
                    gather_table(a, half)
            quantise_w2(0, a)
            if a < PASSES - 1:
                for u in range(EARLY):
                    phase_pass(u, a)
        for half in range(HALVES):
            gather_table(PASSES - 1, half)
        quantise_w2(1, 0)

        vec_turned = psum.tile([P, P], F32, name="vec_turned", tag="turn", bufs=2)
        nc.tensor.transpose(vec_turned[:], vec_rows[:], ident_f32[:])
        vec_cols = keep.tile([P, 3 * TILES], F32, name="vec_cols")
        nc.scalar.copy(vec_cols[:], vec_turned[:, 0 : 3 * TILES])

        w3_codes = keep.tile([P, H], U32, name="w3_codes", align_bytes=64)
        w3_scales = keep.tile([P, H], U8, name="w3_scales", align_bytes=64)
        h = [keep.tile([P, S], F32, name="h%d" % t, align_bytes=64) for t in range(TILES)]
        x_turned = keep.tile([P, M2 // P, 2, P], F32, name="x_turned", tag="x_turned", align_bytes=64)
        turns, whole, cosine = [None] * UNITS, [None] * UNITS, [None] * UNITS
        x_tiles, picked_tiles = [], []

        def count_turns(u):
            for a in range(PASSES - 1 if u < EARLY else 0, PASSES):
                phase_pass(u, a)
            if u in VECTOR_LED:
                whole[u] = ring.tile([P, N], I32, name="whole_signed", tag="whole_signed", align_bytes=64)
                nc.vector.tensor_scalar(whole[u][:], phase[u][:], TURN, 0.25, ALU.mult, ALU.add)
                return
            if u == len(VECTOR_LED):
                turns[u] = keep.tile([P, N], F32, name="turns", tag="w2_raw1_0", align_bytes=64)
            else:
                turns[u] = ring.tile([P, N], F32, name="turns", tag="turns", bufs=3, align_bytes=64)
            nc.scalar.activation(turns[u][:], phase[u][:], ACT.Abs, scale=TURN)
            whole[u] = ring.tile([P, N], U32, name="whole", tag="whole", bufs=3, align_bytes=64)
            nc.scalar.activation(whole[u][:], turns[u][:], ACT.Copy, bias=0.25)

        def take_cosine(u):
            for a in range(PASSES):
                level_pass(u, a)
            frac = keep.tile([P, N], F32, name="frac", tag="frac%d" % u, align_bytes=64)
            if u in (0, UNITS - 1):
                cosine[u] = keep.tile([P, N], F32, name="cosine", tag="cosine%d" % u, align_bytes=64)
            else:
                cosine[u] = ring.tile([P, N], F32, name="cosine", tag="cosine", align_bytes=64)
            if u in VECTOR_LED:
                nc.vector.scalar_tensor_tensor(frac[:], phase[u][:], TURN, whole[u][:], ALU.mult, ALU.subtract)
                nc.scalar.activation(cosine[u][:], frac[:], ACT.Sin, scale=2.0 * math.pi, bias=math.pi / 2.0)
            else:
                nc.vector.scalar_tensor_tensor(
                    frac[:], turns[u][:], 0.25, whole[u][:].bitcast(I32), ALU.add, ALU.subtract
                )
                nc.scalar.activation(cosine[u][:], frac[:], ACT.Sin, scale=2.0 * math.pi)

        def finish_features(u):
            t, half = UNIT_ORDER[u]
            nc.vector.scalar_tensor_tensor(
                h[t][:, N * half : N * (half + 1)], level[u][:], vec_cols[:, t : t + 1], cosine[u][:], ALU.mult, ALU.mult
            )

        def pick_columns(t, tag):
            h_picked = keep.tile([P, M2], F32, name="h_picked", tag=tag, align_bytes=64)
            nc.vector.tensor_copy(h_picked[:], h[t][:].indirect(pos_sb[:]))
            picked_tiles.append(h_picked)

        def take_maximum(t, tag):
            x_rows = keep.tile([P, M2], BF16, name="x_rows", tag=tag, align_bytes=64)
            nc.vector.tensor_tensor(x_rows[:], picked_tiles[t][:], refm_sb[t][:], ALU.max)
            x_tiles.append(x_rows)

        def turn_rows(t, tag, bufs):
            turned = psum.tile([P, M2], BF16, name="turned", tag=tag, bufs=bufs)
            for blk in range(M2 // P):
                cols = slice(P * blk, P * (blk + 1))
                nc.tensor.transpose(turned[:, cols], x_tiles[t][:, cols], ident_bf16[:])
            nc.scalar.copy(
                x_turned[:, :, :, 32 * t : 32 * (t + 1)],
                turned[:].bitcast(F32).rearrange("m (blk p u) -> m blk u p", blk=M2 // P, u=2),
            )

        for step in range(UNITS + 2):
            if step < UNITS:
                count_turns(step)
            if 1 <= step <= UNITS:
                take_cosine(step - 1)
            if step >= 2:
                finish_features(step - 2)
            if step == 3:
                quantise_w2(1, 2, copy=nc.vector.tensor_copy, tag="cosine0")
                quantise_w2(1, 1, tag="frac2")
            if step == 4:
                pick_columns(0, "h_picked0")
                take_maximum(0, "x_rows0")
            if step == 5:
                pick_columns(1, "h_picked1")
                take_maximum(1, "x_rows1")
            if step == 8:
                pick_columns(2, "frac6")
            if step == 9:
                take_maximum(2, "frac7")

        pick_columns(TILES - 1, "h_picked_last")
        take_maximum(TILES - 1, "x_rows_last")
        for t in range(TILES - 1):
            turn_rows(t, bank(UNITS - 3 + t, 0), 1)
        grouped3 = keep.tile([P, H * PACK], BF16, name="grouped3", tag="cosine%d" % (UNITS - 1), align_bytes=64)
        round_and_interleave(nc.scalar.copy, grouped3[:], w3_raw[:])
        nc.vector.quantize_mx(out=w3_codes[:].bitcast(FP8X4), scales=w3_scales[:], in_=grouped3[:])

        turn_rows(TILES - 1, "turn", 2)
        x_codes = keep.tile([P, M2], U32, name="x_codes", align_bytes=64)
        x_scales = keep.tile([P, M2], U8, name="x_scales", align_bytes=64)
        for c in range(2):
            back = psum.tile([P, 2, 2, P], F32, name="back", tag="turn", bufs=2)
            for blk in range(2):
                for u in range(2):
                    nc.tensor.transpose(back[:, blk, u, :], x_turned[:, 2 * c + blk, u, :], ident_f32[:])
            x_words = keep.tile([P, M2], F32, name="x_words", tag="x_words%d" % c, align_bytes=64)
            nc.scalar.copy(
                x_words[:].rearrange("p (blk m u) -> p blk m u", blk=2, u=2),
                back[:].rearrange("p blk u m -> p blk m u"),
            )
            cols = slice(M2 // 2 * c, M2 // 2 * (c + 1))
            nc.vector.quantize_mx(
                out=x_codes[:, cols].bitcast(FP8X4), scales=x_scales[:, cols], in_=x_words[:].bitcast(BF16)
            )

        base = []
        last = TILES - 1
        for t, tag in enumerate(("h_picked_last", "refm%d" % last, "x_rows_last", "x_words1")):
            page = keep.tile([P, S], F32, name="base%d" % t, tag=tag, align_bytes=64)
            nc.vector.scalar_tensor_tensor(
                page[:], h[t][:], vec_cols[:, TILES + t : TILES + t + 1], offm_sb[t][:], ALU.mult, ALU.add
            )
            base.append(page)
        for t in range(TILES):
            acc = psum.tile([P, M2], F32, name="acc", tag=bank(UNITS - 4 + t, 1))
            nc.tensor.matmul_mx(
                out=acc[:],
                lhsT=w3_codes[:, P * t : P * (t + 1)].bitcast(FP8X4),
                lhsT_scale=w3_scales[:, P * t : P * (t + 1)],
                rhs=x_codes[:].bitcast(FP8X4),
                rhs_scale=x_scales[:],
                start=True,
                stop=True,
            )
            y = ring.tile([P, M2], F32, name="y", tag="y", bufs=4, align_bytes=64)
            nc.scalar.activation(y[:], acc[:], ACT.Tanh, bias=vec_cols[:, 2 * TILES + t : 2 * TILES + t + 1])
            nc.vector.tensor_tensor(base[t][:].indirect(pos_sb[:]), y[:], wgo_sb[:], ALU.mult)
            nc.sync.dma_start(out[P * t : P * (t + 1), :], base[t][:])
